import numpy as np
import ml_dtypes


def mxq(x, axis, fmt="e4m3"):
    dtype, down = {"e4m3": (ml_dtypes.float8_e4m3fn, 7), "e5m2": (ml_dtypes.float8_e5m2, 14)}[fmt]
    v = np.moveaxis(np.asarray(x, np.float32).astype(ml_dtypes.bfloat16).astype(np.float64), axis, -1)
    blocks = v.reshape(v.shape[:-1] + (-1, 32))
    amax = np.abs(blocks).max(-1, keepdims=True)
    byte = np.maximum(np.where(amax > 0, np.frexp(amax)[1] - 1 + 127, 0) - down, 1)
    scale = np.exp2(byte - 127.0)
    codes = (blocks / scale).astype(np.float32).astype(dtype).astype(np.float64)
    return np.moveaxis((codes * scale).reshape(v.shape), -1, axis)


WIDE = False


def mx_kscale(k):
    if not WIDE:
        return np.ones(k)
    levels = np.array([30, -30])
    if k % 512:
        return np.exp2(np.random.permutation(np.resize(levels, k // 32))).repeat(32)
    a = np.empty((k // 512, 16))
    for p in range(k // 512):
        a[p, :8] = np.random.permutation(np.resize(levels, 8))
        for g in range(8):
            far = levels[np.abs(levels - a[p, g]) >= 10]
            a[p, g + 8] = far[np.random.randint(len(far))]
    return np.exp2(a.ravel()).repeat(32)


def f64(x):
    return np.asarray(x).astype(np.float64)


def striped(idx):
    return np.tile(np.asarray(idx).reshape(-1, 16).T, (8, 1)).astype(np.uint16)


def unstriped(offs):
    return offs[:16].T.reshape(-1).astype(np.int64)


E2M1 = np.array([0.0, 0.5, 1.0, 1.5, 2.0, 3.0, 4.0, 6.0, -0.0, -0.5, -1.0, -1.5, -2.0, -3.0, -4.0, -6.0])


def pack_weight(w, fmt):
    k, n = w.shape
    w = f64(np.asarray(w, np.float32).astype(ml_dtypes.bfloat16)).reshape(k // 32, 32, n)
    amax = np.abs(w).max(1)
    if fmt in ("e4m3", "e5m2"):
        byte = np.frexp(amax)[1] - 1 + 127 - (7 if fmt == "e4m3" else 14)
    else:
        mant, ex = np.frexp(amax / 6.0)
        byte = np.where(mant > 0.5, ex, ex - 1) + 127
    byte = np.clip(np.where(amax > 0, byte, 1), 1, 254)
    scaled = (w * np.exp2(127.0 - byte)[:, None, :]).reshape(k, n).astype(np.float32)
    by_word = np.ascontiguousarray(scaled.reshape(k // 512, 128, 4, n).transpose(0, 1, 3, 2))
    if fmt in ("e4m3", "e5m2"):
        words = by_word.astype(ml_dtypes.float8_e4m3fn if fmt == "e4m3" else ml_dtypes.float8_e5m2).view(np.uint8)
    else:
        c = by_word.astype(ml_dtypes.float4_e2m1fn).view(np.uint8) & 0xF
        words = (c[..., 0::2] | (c[..., 1::2] << 4)).reshape(k // 512, 128, 2 * n)
    return np.ascontiguousarray(words), np.ascontiguousarray(byte.astype(np.uint8).reshape(k // 512, 16, n))


def unpack_weight(words, scales, fmt):
    g, _, n = scales.shape
    words = np.ascontiguousarray(words).reshape(g, 128, n, -1)
    if fmt in ("e4m3", "e5m2"):
        vals = words.view(ml_dtypes.float8_e4m3fn if fmt == "e4m3" else ml_dtypes.float8_e5m2).astype(np.float64)
    else:
        nib = np.empty((g, 128, n, 4), np.uint8)
        nib[..., 0::2] = words & 0xF
        nib[..., 1::2] = words >> 4
        vals = E2M1[nib]
    vals = vals * np.repeat(np.exp2(scales.astype(np.float64) - 127.0), 8, axis=1)[..., None]
    return vals.transpose(0, 1, 3, 2).reshape(g * 512, n)


def sigmoid(v):
    return 1.0 / (1.0 + np.exp(-v))


def sgn(shape):
    return np.random.uniform(0.5, 2.0, shape) * np.where(np.random.standard_normal(shape) < 0, -1.0, 1.0)


K, T, J, R, F, Z, N, C, O = 512, 1024, 256, 512, 512, 1024, 256, 512, 128


def setup_inputs():
    n = np.random.standard_normal
    idx = np.random.permutation(T)[:J]
    idx2 = np.random.permutation(Z)[:J]
    idx3 = np.random.permutation(C)[:J]
    idx4 = np.random.permutation(C)[:J]
    idx5 = np.random.permutation(J)[:O]
    idx6 = np.random.permutation(J)[:O]
    fk = mx_kscale(K)
    ff = mx_kscale(F)
    fr = mx_kscale(R)
    xtp = pack_weight(n((K, T)) / fk[:, None], "e4m3")
    xop = pack_weight(n((F, Z)) / ff[:, None], "e2m1")
    wp = pack_weight(n((K, R)) * 1 / np.sqrt(K) * fk[:, None] * fr, "e2m1")
    w2p = pack_weight(n((K, R)) * 1 / np.sqrt(K) * fk[:, None] * fr, "e5m2")
    w0p = pack_weight(n((F, R)) * 1 / np.sqrt(F) * ff[:, None] * fr, "e5m2")
    wbp = pack_weight(n((R, N)) * 1 / np.sqrt(R) / fr[:, None], "e5m2")
    wcp = pack_weight(n((R, N)) * 1 / np.sqrt(R) / fr[:, None], "e2m1")
    return {
        "xt_words": xtp[0],
        "xt_scales": xtp[1],
        "xo_words": xop[0],
        "xo_scales": xop[1],
        "w_words": wp[0],
        "w_scales": wp[1],
        "w2_words": w2p[0],
        "w2_scales": w2p[1],
        "w0_words": w0p[0],
        "w0_scales": w0p[1],
        "wb_words": wbp[0],
        "wb_scales": wbp[1],
        "wc_words": wcp[0],
        "wc_scales": wcp[1],
        "so": (np.random.uniform(0.5, 1.6, (N, 1))).astype(np.float32),
        "sp": (sgn((N, 1))).astype(np.float32),
        "bo": (np.random.uniform(-2.0, 2.0, (N, 1))).astype(np.float32),
        "offs": striped(idx),
        "offs2": striped(idx2),
        "offs3": striped(idx3),
        "offs4": striped(idx4),
        "offs5": striped(idx5),
        "offs6": striped(idx6),
    }


def reference(xt_words, xt_scales, xo_words, xo_scales, w_words, w_scales, w2_words, w2_scales, w0_words, w0_scales, wb_words, wb_scales, wc_words, wc_scales, so, sp, bo, offs, offs2, offs3, offs4, offs5, offs6):
    idx = unstriped(offs)
    idx2 = unstriped(offs2)
    idx3 = unstriped(offs3)
    idx4 = unstriped(offs4)
    idx5 = unstriped(offs5)
    idx6 = unstriped(offs6)
    xtu = unpack_weight(xt_words, xt_scales, "e4m3")
    xou = unpack_weight(xo_words, xo_scales, "e2m1")
    wu = unpack_weight(w_words, w_scales, "e2m1")
    w2u = unpack_weight(w2_words, w2_scales, "e5m2")
    w0u = unpack_weight(w0_words, w0_scales, "e5m2")
    wbu = unpack_weight(wb_words, wb_scales, "e5m2")
    wcu = unpack_weight(wc_words, wc_scales, "e2m1")
    xtidxg = xtu[:, idx]
    a = wu.T @ xtidxg
    xoidx2g = xou[:, idx2]
    b = w2u.T @ xtidxg + w0u.T @ xoidx2g
    hid = np.maximum(a, b)
    hidq = mxq(hid, 0, "e4m3")
    p = wbu.T @ hidq
    q = wcu.T @ hidq
    pw = np.zeros((N, C))
    pw[:, idx3] = p
    m0 = np.maximum(pw[:, idx4], q)
    y = m0[:, idx5] * f64(so) * sigmoid(m0[:, idx6] * f64(sp) + f64(bo))
    return y

@@ -1,0 +1,233 @@
+from contextlib import ExitStack
+
+import concourse.mybir as mybir
+from concourse.masks import make_identity
+
+K, T, J, R, F, Z, N, C, O = 512, 1024, 256, 512, 512, 1024, 256, 512, 128
+FLOPS = 2 * (K * R * J * 2 + F * R * J + R * N * J * 2)
+
+F32 = mybir.dt.float32
+BF16 = mybir.dt.bfloat16
+I32 = mybir.dt.int32
+U32 = mybir.dt.uint32
+U16 = mybir.dt.uint16
+U8 = mybir.dt.uint8
+E4M3 = mybir.dt.float8_e4m3fn_x4
+E5M2 = mybir.dt.float8_e5m2_x4
+E2M1 = mybir.dt.float4_e2m1fn_x4
+ACT = mybir.ActivationFunctionType
+ALU = mybir.AluOpType
+
+P = 128
+HALVES = J // P
+ROW_TILES = N // P
+
+
+def tile_list_outcomegatedchain_leaned_kernel(
+    tc, xt_words, xt_scales, xo_words, xo_scales, w_words, w_scales, w2_words, w2_scales,
+    w0_words, w0_scales, wb_words, wb_scales, wc_words, wc_scales, so, sp, bo,
+    offs, offs2, offs3, offs4, offs5, offs6, out,
+):
+    nc = tc.nc
+    with ExitStack() as ctx:
+        lists = ctx.enter_context(tc.tile_pool(name="lists", bufs=1))
+        keep = ctx.enter_context(tc.tile_pool(name="keep", bufs=1))
+        psum = ctx.enter_context(tc.psum_pool(name="psum", bufs=1))
+
+        def tile(shape, dtype, name):
+            return keep.tile(shape, dtype, name=name, align_bytes=64)
+
+        def load_list(src, name):
+            dst = lists.tile(list(src.shape), U16, name=name)
+            nc.sync.dma_start(dst[:], src)
+            return dst
+
+        def load_words(queue, src, width, dtype, name):
+            rows = src[0]
+            if len(rows.shape) == 3:
+                rows = rows.rearrange("p n t -> p (n t)")
+            dst = tile([P, width], dtype, name)
+            queue.dma_start(dst[:].bitcast(I32), rows.bitcast(I32))
+            return dst
+
+        def load_scale_rows(queue, plane, src, col0, width, s, base=64):
+            rows = src[0].bitcast(I32).rearrange("(c s r) n -> s r c n", c=2, s=2)
+            p0 = base + 32 * s
+            queue.dma_start(plane[p0 : p0 + 4, :, col0 : col0 + width].bitcast(I32), rows[s])
+
+        def load_scale_pairs(queue, plane, src, col0, width, base=64):
+            for s in range(2):
+                load_scale_rows(queue, plane, src, col0, width, s, base)
+
+        def spread_scale_pairs(plane, col0, width):
+            nc.vector.tensor_copy(
+                plane[0:64, 1, col0 : col0 + width].bitcast(I32),
+                plane[64:128, 0, col0 : col0 + width].bitcast(I32),
+            )
+
+        def load_column(src, name):
+            dst = tile([P, ROW_TILES], F32, name)
+            with nc.allow_non_contiguous_dma(reason="one value a partition"):
+                nc.gpsimd.dma_start(dst[:], src.rearrange("(c p) o -> p (c o)", p=P))
+            return dst
+
+        plane_w = tile([P, 2, R], U8, "plane_w")
+        plane_b = tile([P, 2, 2 * R], U8, "plane_b")
+        plane_c = tile([P, 2, 2 * N], U8, "plane_c")
+        xt_stage = keep.tile([P, 2, T], U8, name="xt_stage", tag="xt_stage", align_bytes=64)
+        xo_stage = keep.tile([P, 2, Z], U8, name="xo_stage", tag="xo_stage", align_bytes=64)
+        xt_plane = tile([P, T], U8, "xt_plane")
+        xo_plane = tile([P, Z], U8, "xo_plane")
+        board = [tile([P, C], F32, "board%d" % n) for n in range(ROW_TILES)]
+        ident = tile([P, P], F32, "ident")
+        nc.vector.memset(xt_stage[0:64, 0, :].bitcast(I32), 0)
+        nc.gpsimd.memset(xt_stage[0:64, 1, :].bitcast(I32), 0)
+        nc.vector.memset(plane_w[64:128].bitcast(I32), 0)
+        nc.vector.memset(plane_b[64:128, :, 0:R].bitcast(I32), 0)
+        nc.gpsimd.memset(plane_b[64:128, :, R : 2 * R].bitcast(I32), 0)
+        nc.vector.memset(xo_stage[0:64].bitcast(I32), 0)
+        nc.vector.memset(plane_c[64:128].bitcast(I32), 0)
+        nc.vector.memset(board[0][:], 0.0)
+        load_scale_pairs(nc.gpsimd, plane_b, w0_scales, R, R)
+        make_identity(nc, ident[:])
+        nc.gpsimd.memset(board[1][:], 0.0)
+        sp_col = load_column(sp, "sp_col")
+        bo_col = load_column(bo, "bo_col")
+        so_col = load_column(so, "so_col")
+
+        idx = load_list(offs, "idx")
+        idx2 = load_list(offs2, "idx2")
+        load_scale_pairs(nc.sync, xt_stage, xt_scales, 0, T, base=0)
+        load_scale_pairs(nc.sync, plane_b, w2_scales, 0, R)
+        load_scale_pairs(nc.sync, xo_stage, xo_scales, 0, Z, base=0)
+        load_scale_pairs(nc.sync, plane_c, wb_scales, 0, N)
+        load_scale_pairs(nc.sync, plane_c, wc_scales, N, N)
+        xt_tab = load_words(nc.scalar, xt_words, T, U32, "xt_tab")
+        load_scale_pairs(nc.scalar, plane_w, w_scales, 0, R)
+        w_tab = load_words(nc.scalar, w_words, 2 * R, U8, "w_tab")
+        xo_tab = load_words(nc.scalar, xo_words, Z, U16, "xo_tab")
+        w2_tab = load_words(nc.scalar, w2_words, R, U32, "w2_tab")
+        w0_tab = load_words(nc.scalar, w0_words, R, U32, "w0_tab")
+        wb_tab = load_words(nc.sync, wb_words, N, U32, "wb_tab")
+        idx3 = load_list(offs3, "idx3")
+        wc_tab = load_words(nc.sync, wc_words, 2 * N, U8, "wc_tab")
+        idx4 = load_list(offs4, "idx4")
+        idx6 = load_list(offs6, "idx6")
+        idx5 = load_list(offs5, "idx5")
+
+        def spread_table_scales(plane, stage):
+            for c in range(2):
+                nc.vector.tensor_copy(plane[64 * c : 64 * c + 64, :].bitcast(I32), stage[0:64, c, :].bitcast(I32))
+
+        spread_table_scales(xt_plane, xt_stage)
+        xt_both = keep.tile([P, J], U32, name="xt_both", tag="xt_stage", align_bytes=64)
+        xt_codes = [xt_both[:, h * P : (h + 1) * P] for h in range(HALVES)]
+        xt_bytes = [tile([P, P], U8, "xt_bytes%d" % h) for h in range(HALVES)]
+        xo_bytes = [tile([P, P], U8, "xo_bytes%d" % h) for h in range(HALVES)]
+
+        def half(lst, h):
+            return lst[:, 8 * h : 8 * h + 8]
+
+        bank_a = [psum.tile([P, R], F32, name="bank_a%d" % h) for h in range(HALVES)]
+        bank_b = [psum.tile([P, R], F32, name="bank_b%d" % h) for h in range(HALVES)]
+        bank_p = [psum.tile([P, J], F32, name="bank_p%d" % n) for n in range(ROW_TILES)]
+        bank_q = [psum.tile([P, J], F32, name="bank_q%d" % n) for n in range(ROW_TILES)]
+        a_rows = [tile([P, R], F32, "a_rows%d" % h) for h in range(HALVES)]
+
+        def by_word_planes(bank):
+            return bank[:].rearrange("j (p u e) -> j u p e", u=2, e=2)
+
+        def as_word_planes(t):
+            return t[:].rearrange("j (u p e) -> j u p e", u=2, e=2)
+
+        for h in range(HALVES):
+            nc.vector.tensor_copy(xt_bytes[h][:], xt_plane[:].indirect(half(idx, h)))
+            nc.vector.tensor_copy(xt_codes[h], xt_tab[:].indirect(half(idx, h)))
+            if h == 0:
+                spread_scale_pairs(plane_w, 0, R)
+            nc.tensor.matmul_mx(
+                bank_a[h][:], lhsT=xt_codes[h].bitcast(E4M3), lhsT_scale=xt_bytes[h][:],
+                rhs=w_tab[:].bitcast(E2M1), rhs_scale=plane_w[:, 1, 0:R], start=True, stop=True,
+            )
+            nc.scalar.copy(as_word_planes(a_rows[h]), by_word_planes(bank_a[h]))
+        spread_scale_pairs(plane_b, 0, 2 * R)
+        xo_codes = [tile([P, P], U16, "xo_codes0")]
+        nc.vector.tensor_copy(xo_codes[0][:], xo_tab[:].indirect(half(idx2, 0)))
+        spread_table_scales(xo_plane, xo_stage)
+        xo_codes.append(keep.tile([P, P], U16, name="xo_codes1", tag="xo_stage", align_bytes=64))
+        for h in range(HALVES):
+            nc.tensor.matmul_mx(
+                bank_b[h][:], lhsT=xt_codes[h].bitcast(E4M3), lhsT_scale=xt_bytes[h][:],
+                rhs=w2_tab[:].bitcast(E5M2), rhs_scale=plane_b[:, 1, 0:R], start=True, stop=False,
+            )
+        for h in range(HALVES):
+            nc.vector.tensor_copy(xo_bytes[h][:], xo_plane[:].indirect(half(idx2, h)))
+            if h == 1:
+                nc.vector.tensor_copy(xo_codes[h][:], xo_tab[:].indirect(half(idx2, h)))
+            nc.tensor.matmul_mx(
+                bank_b[h][:], lhsT=xo_codes[h][:].bitcast(E2M1), lhsT_scale=xo_bytes[h][:],
+                rhs=w0_tab[:].bitcast(E5M2), rhs_scale=plane_b[:, 1, R : 2 * R], start=False, stop=True,
+            )
+
+        hid_rows = [tile([P, R], BF16, "hid_rows%d" % h) for h in range(HALVES)]
+        hid_cols = [tile([P, R], BF16, "hid_cols%d" % h) for h in range(HALVES)]
+        hid_codes = [tile([P, P], U32, "hid_codes%d" % h) for h in range(HALVES)]
+        hid_bytes = [tile([P, P], U8, "hid_bytes%d" % h) for h in range(HALVES)]
+        for h in range(HALVES):
+            words = hid_rows[h][:].bitcast(F32)
+            for u in range(2):
+                nc.vector.tensor_tensor(
+                    as_word_planes(hid_rows[h])[:, u], by_word_planes(bank_b[h])[:, u],
+                    as_word_planes(a_rows[h])[:, u], ALU.max,
+                )
+                nc.tensor.transpose(bank_a[h][:, u * P : (u + 1) * P], words[:, u * P : (u + 1) * P], ident[:])
+            nc.scalar.copy(
+                hid_cols[h][:].bitcast(F32).rearrange("p (j u) -> p j u", u=2),
+                bank_a[h][:, 0 : 2 * P].rearrange("p (u j) -> p j u", u=2),
+            )
+        spread_scale_pairs(plane_c, 0, 2 * N)
+
+        p_rows = [tile([P, J], F32, "p_rows%d" % n) for n in range(ROW_TILES)]
+        for h in range(HALVES):
+            cols = slice(h * P, (h + 1) * P)
+            nc.vector.quantize_mx(out=hid_codes[h][:].bitcast(E4M3), scales=hid_bytes[h][:], in_=hid_cols[h][:])
+            for n in range(ROW_TILES):
+                nc.tensor.matmul_mx(
+                    bank_p[n][:, cols], lhsT=wb_tab[:, n * P : (n + 1) * P].bitcast(E5M2),
+                    lhsT_scale=plane_c[:, 1, n * P : (n + 1) * P],
+                    rhs=hid_codes[h][:].bitcast(E4M3), rhs_scale=hid_bytes[h][:], start=True, stop=True,
+                )
+            nc.vector.tensor_copy(p_rows[0][:, cols], bank_p[0][:, cols])
+            nc.scalar.copy(p_rows[1][:, cols], bank_p[1][:, cols])
+            for n in range(ROW_TILES):
+                nc.tensor.matmul_mx(
+                    bank_q[n][:, cols], lhsT=wc_tab[:, 2 * n * P : 2 * (n + 1) * P].bitcast(E2M1),
+                    lhsT_scale=plane_c[:, 1, N + n * P : N + (n + 1) * P],
+                    rhs=hid_codes[h][:].bitcast(E4M3), rhs_scale=hid_bytes[h][:], start=True, stop=True,
+                )
+        for h in range(HALVES):
+            cols = slice(h * P, (h + 1) * P)
+            nc.vector.tensor_copy(board[0][:].indirect(half(idx3, h)), p_rows[0][:, cols])
+            nc.scalar.activation(board[1][:].indirect(half(idx3, h)), p_rows[1][:, cols], ACT.Copy)
+
+        picked = [tile([P, J], F32, "picked%d" % n) for n in range(ROW_TILES)]
+        kept = [tile([P, J], F32, "kept%d" % n) for n in range(ROW_TILES)]
+        for h in range(HALVES):
+            cols = slice(h * P, (h + 1) * P)
+            nc.vector.tensor_copy(picked[0][:, cols], board[0][:].indirect(half(idx4, h)))
+        nc.scalar.activation(picked[1][:], board[1][:].indirect(idx4[:]), ACT.Copy)
+        for h in range(HALVES):
+            cols = slice(h * P, (h + 1) * P)
+            nc.vector.tensor_tensor(kept[0][:, cols], picked[0][:, cols], bank_q[0][:, cols], ALU.max)
+        nc.vector.tensor_tensor(kept[1][:], picked[1][:], bank_q[1][:], ALU.max)
+        for n in range(ROW_TILES):
+            gate = tile([P, O], F32, "gate%d" % n)
+            scaled = tile([P, O], F32, "scaled%d" % n)
+            result = tile([P, O], F32, "result%d" % n)
+            nc.scalar.activation(
+                gate[:], kept[n][:].indirect(idx6[:]), ACT.Sigmoid,
+                bias=bo_col[:, n : n + 1], scale=sp_col[:, n : n + 1],
+            )
+            nc.scalar.activation(scaled[:], kept[n][:].indirect(idx5[:]), ACT.Copy, scale=so_col[:, n : n + 1])
+            nc.vector.tensor_tensor(result[:], scaled[:], gate[:], ALU.mult)
+            nc.sync.dma_start(out[n * P : (n + 1) * P, :], result[:])

@@ -80,6 +80,8 @@ def tile_list_outcomegatedchain_leaned_kernel(
         xo_plane = tile([P, Z], U8, "xo_plane")
         board = [tile([P, C], F32, "board%d" % n) for n in range(ROW_TILES)]
         ident = tile([P, P], F32, "ident")
+        warm_in = tile([P, 1], F32, "warm_in")
+        warm_out = tile([P, 1], F32, "warm_out")
         nc.vector.memset(xt_stage[0:64, 0, :].bitcast(I32), 0)
         nc.gpsimd.memset(xt_stage[0:64, 1, :].bitcast(I32), 0)
         nc.vector.memset(plane_w[64:128].bitcast(I32), 0)
@@ -88,6 +90,7 @@ def tile_list_outcomegatedchain_leaned_kernel(
         nc.vector.memset(xo_stage[0:64].bitcast(I32), 0)
         nc.vector.memset(plane_c[64:128].bitcast(I32), 0)
         nc.vector.memset(board[0][:], 0.0)
+        nc.vector.memset(warm_in[:], 0.0)
         load_scale_pairs(nc.gpsimd, plane_b, w0_scales, R, R)
         make_identity(nc, ident[:])
         nc.gpsimd.memset(board[1][:], 0.0)
@@ -108,6 +111,7 @@ def tile_list_outcomegatedchain_leaned_kernel(
         xo_tab = load_words(nc.scalar, xo_words, Z, U16, "xo_tab")
         w2_tab = load_words(nc.scalar, w2_words, R, U32, "w2_tab")
         w0_tab = load_words(nc.scalar, w0_words, R, U32, "w0_tab")
+        nc.scalar.activation(warm_out[:], warm_in[:], ACT.Sigmoid)
         wb_tab = load_words(nc.sync, wb_words, N, U32, "wb_tab")
         idx3 = load_list(offs3, "idx3")
         wc_tab = load_words(nc.sync, wc_words, 2 * N, U8, "wc_tab")

@@ -68,13 +68,13 @@ def tile_list_outcomegatedchain_leaned_kernel(
         def load_column(src, name):
             dst = tile([P, ROW_TILES], F32, name)
             with nc.allow_non_contiguous_dma(reason="one value a partition"):
-                nc.gpsimd.dma_start(dst[:], src.rearrange("(c p) o -> p (c o)", p=P))
+                nc.sync.dma_start(dst[:], src.rearrange("(c p) o -> p (c o)", p=P))
             return dst
 
         plane_w = tile([P, 2, R], U8, "plane_w")
         plane_b = tile([P, 2, 2 * R], U8, "plane_b")
         plane_c = tile([P, 2, 2 * N], U8, "plane_c")
-        xt_stage = keep.tile([P, 2, T], U8, name="xt_stage", tag="xt_stage", align_bytes=64)
+        xt_stage = tile([P, 2, T], U8, "xt_stage")
         xo_stage = keep.tile([P, 2, Z], U8, name="xo_stage", tag="xo_stage", align_bytes=64)
         xt_plane = tile([P, T], U8, "xt_plane")
         xo_plane = tile([P, Z], U8, "xo_plane")
@@ -85,47 +85,48 @@ def tile_list_outcomegatedchain_leaned_kernel(
         nc.vector.memset(xt_stage[0:64, 0, :].bitcast(I32), 0)
         nc.gpsimd.memset(xt_stage[0:64, 1, :].bitcast(I32), 0)
         nc.vector.memset(plane_w[64:128].bitcast(I32), 0)
-        nc.vector.memset(plane_b[64:128, :, 0:R].bitcast(I32), 0)
         nc.gpsimd.memset(plane_b[64:128, :, R : 2 * R].bitcast(I32), 0)
+        nc.vector.memset(plane_b[64:128, :, 0:R].bitcast(I32), 0)
         nc.vector.memset(xo_stage[0:64].bitcast(I32), 0)
-        nc.vector.memset(plane_c[64:128].bitcast(I32), 0)
         nc.vector.memset(board[0][:], 0.0)
         nc.vector.memset(warm_in[:], 0.0)
-        load_scale_pairs(nc.gpsimd, plane_b, w0_scales, R, R)
+        load_scale_rows(nc.gpsimd, plane_b, w0_scales, R, R, 1)
+        nc.gpsimd.memset(plane_c[64:128].bitcast(I32), 0)
         make_identity(nc, ident[:])
         nc.gpsimd.memset(board[1][:], 0.0)
-        sp_col = load_column(sp, "sp_col")
-        bo_col = load_column(bo, "bo_col")
-        so_col = load_column(so, "so_col")
+        nc.scalar.activation(warm_out[:], warm_in[:], ACT.Sigmoid)
 
         idx = load_list(offs, "idx")
-        idx2 = load_list(offs2, "idx2")
+        w_tab = load_words(nc.sync, w_words, 2 * R, U8, "w_tab")
         load_scale_pairs(nc.sync, xt_stage, xt_scales, 0, T, base=0)
-        load_scale_pairs(nc.sync, plane_b, w2_scales, 0, R)
+        load_scale_pairs(nc.sync, plane_w, w_scales, 0, R)
+        load_scale_rows(nc.sync, plane_b, w2_scales, 0, R, 0)
+        xt_tab = load_words(nc.sync, xt_words, T, U32, "xt_tab")
+        load_scale_rows(nc.sync, plane_b, w2_scales, 0, R, 1)
+        xo_tab = load_words(nc.sync, xo_words, Z, U16, "xo_tab")
+        load_scale_rows(nc.sync, plane_b, w0_scales, R, R, 0)
+        idx2 = load_list(offs2, "idx2")
+        w2_tab = load_words(nc.sync, w2_words, R, U32, "w2_tab")
         load_scale_pairs(nc.sync, xo_stage, xo_scales, 0, Z, base=0)
+        w0_tab = load_words(nc.sync, w0_words, R, U32, "w0_tab")
         load_scale_pairs(nc.sync, plane_c, wb_scales, 0, N)
         load_scale_pairs(nc.sync, plane_c, wc_scales, N, N)
-        xt_tab = load_words(nc.scalar, xt_words, T, U32, "xt_tab")
-        load_scale_pairs(nc.scalar, plane_w, w_scales, 0, R)
-        w_tab = load_words(nc.scalar, w_words, 2 * R, U8, "w_tab")
-        xo_tab = load_words(nc.scalar, xo_words, Z, U16, "xo_tab")
-        w2_tab = load_words(nc.scalar, w2_words, R, U32, "w2_tab")
-        w0_tab = load_words(nc.scalar, w0_words, R, U32, "w0_tab")
-        nc.scalar.activation(warm_out[:], warm_in[:], ACT.Sigmoid)
         wb_tab = load_words(nc.sync, wb_words, N, U32, "wb_tab")
         idx3 = load_list(offs3, "idx3")
         wc_tab = load_words(nc.sync, wc_words, 2 * N, U8, "wc_tab")
-        idx4 = load_list(offs4, "idx4")
         idx6 = load_list(offs6, "idx6")
+        sp_col = load_column(sp, "sp_col")
+        bo_col = load_column(bo, "bo_col")
         idx5 = load_list(offs5, "idx5")
+        so_col = load_column(so, "so_col")
+        idx4 = load_list(offs4, "idx4")
 
         def spread_table_scales(plane, stage):
             for c in range(2):
                 nc.vector.tensor_copy(plane[64 * c : 64 * c + 64, :].bitcast(I32), stage[0:64, c, :].bitcast(I32))
 
         spread_table_scales(xt_plane, xt_stage)
-        xt_both = keep.tile([P, J], U32, name="xt_both", tag="xt_stage", align_bytes=64)
-        xt_codes = [xt_both[:, h * P : (h + 1) * P] for h in range(HALVES)]
+        xt_codes = [tile([P, P], U32, "xt_codes%d" % h) for h in range(HALVES)]
         xt_bytes = [tile([P, P], U8, "xt_bytes%d" % h) for h in range(HALVES)]
         xo_bytes = [tile([P, P], U8, "xo_bytes%d" % h) for h in range(HALVES)]
 
@@ -146,11 +147,11 @@ def tile_list_outcomegatedchain_leaned_kernel(
 
         for h in range(HALVES):
             nc.vector.tensor_copy(xt_bytes[h][:], xt_plane[:].indirect(half(idx, h)))
-            nc.vector.tensor_copy(xt_codes[h], xt_tab[:].indirect(half(idx, h)))
+            nc.vector.tensor_copy(xt_codes[h][:], xt_tab[:].indirect(half(idx, h)))
             if h == 0:
                 spread_scale_pairs(plane_w, 0, R)
             nc.tensor.matmul_mx(
-                bank_a[h][:], lhsT=xt_codes[h].bitcast(E4M3), lhsT_scale=xt_bytes[h][:],
+                bank_a[h][:], lhsT=xt_codes[h][:].bitcast(E4M3), lhsT_scale=xt_bytes[h][:],
                 rhs=w_tab[:].bitcast(E2M1), rhs_scale=plane_w[:, 1, 0:R], start=True, stop=True,
             )
             nc.scalar.copy(as_word_planes(a_rows[h]), by_word_planes(bank_a[h]))
@@ -161,7 +162,7 @@ def tile_list_outcomegatedchain_leaned_kernel(
         xo_codes.append(keep.tile([P, P], U16, name="xo_codes1", tag="xo_stage", align_bytes=64))
         for h in range(HALVES):
             nc.tensor.matmul_mx(
-                bank_b[h][:], lhsT=xt_codes[h].bitcast(E4M3), lhsT_scale=xt_bytes[h][:],
+                bank_b[h][:], lhsT=xt_codes[h][:].bitcast(E4M3), lhsT_scale=xt_bytes[h][:],
                 rhs=w2_tab[:].bitcast(E5M2), rhs_scale=plane_b[:, 1, 0:R], start=True, stop=False,
             )
         for h in range(HALVES):
@@ -216,14 +217,11 @@ def tile_list_outcomegatedchain_leaned_kernel(
 
         picked = [tile([P, J], F32, "picked%d" % n) for n in range(ROW_TILES)]
         kept = [tile([P, J], F32, "kept%d" % n) for n in range(ROW_TILES)]
-        for h in range(HALVES):
-            cols = slice(h * P, (h + 1) * P)
-            nc.vector.tensor_copy(picked[0][:, cols], board[0][:].indirect(half(idx4, h)))
-        nc.scalar.activation(picked[1][:], board[1][:].indirect(idx4[:]), ACT.Copy)
-        for h in range(HALVES):
-            cols = slice(h * P, (h + 1) * P)
-            nc.vector.tensor_tensor(kept[0][:, cols], picked[0][:, cols], bank_q[0][:, cols], ALU.max)
-        nc.vector.tensor_tensor(kept[1][:], picked[1][:], bank_q[1][:], ALU.max)
+        for n in range(ROW_TILES):
+            nc.vector.tensor_copy(picked[n][:, 0:P], board[n][:].indirect(half(idx4, 0)))
+            nc.scalar.activation(picked[n][:, P:J], board[n][:].indirect(half(idx4, 1)), ACT.Copy)
+        for n in range(ROW_TILES):
+            nc.vector.tensor_tensor(kept[n][:], picked[n][:], bank_q[n][:], ALU.max)
         for n in range(ROW_TILES):
             gate = tile([P, O], F32, "gate%d" % n)
             scaled = tile([P, O], F32, "scaled%d" % n)

from contextlib import ExitStack

import concourse.mybir as mybir
from concourse.masks import make_identity

K, T, J, R, F, Z, N, C, O = 512, 1024, 256, 512, 512, 1024, 256, 512, 128
FLOPS = 2 * (K * R * J * 2 + F * R * J + R * N * J * 2)

F32 = mybir.dt.float32
BF16 = mybir.dt.bfloat16
I32 = mybir.dt.int32
U32 = mybir.dt.uint32
U16 = mybir.dt.uint16
U8 = mybir.dt.uint8
E4M3 = mybir.dt.float8_e4m3fn_x4
E5M2 = mybir.dt.float8_e5m2_x4
E2M1 = mybir.dt.float4_e2m1fn_x4
ACT = mybir.ActivationFunctionType
ALU = mybir.AluOpType

P = 128
HALVES = J // P
ROW_TILES = N // P


def tile_list_outcomegatedchain_leaned_kernel(
    tc, xt_words, xt_scales, xo_words, xo_scales, w_words, w_scales, w2_words, w2_scales,
    w0_words, w0_scales, wb_words, wb_scales, wc_words, wc_scales, so, sp, bo,
    offs, offs2, offs3, offs4, offs5, offs6, out,
):
    nc = tc.nc
    with ExitStack() as ctx:
        lists = ctx.enter_context(tc.tile_pool(name="lists", bufs=1))
        keep = ctx.enter_context(tc.tile_pool(name="keep", bufs=1))
        psum = ctx.enter_context(tc.psum_pool(name="psum", bufs=1))

        def tile(shape, dtype, name):
            return keep.tile(shape, dtype, name=name, align_bytes=64)

        def load_list(src, name):
            dst = lists.tile(list(src.shape), U16, name=name)
            nc.sync.dma_start(dst[:], src)
            return dst

        def load_words(queue, src, width, dtype, name):
            rows = src[0]
            if len(rows.shape) == 3:
                rows = rows.rearrange("p n t -> p (n t)")
            dst = tile([P, width], dtype, name)
            queue.dma_start(dst[:].bitcast(I32), rows.bitcast(I32))
            return dst

        def load_scale_rows(queue, plane, src, col0, width, s, base=64):
            rows = src[0].bitcast(I32).rearrange("(c s r) n -> s r c n", c=2, s=2)
            p0 = base + 32 * s
            queue.dma_start(plane[p0 : p0 + 4, :, col0 : col0 + width].bitcast(I32), rows[s])

        def load_scale_pairs(queue, plane, src, col0, width, base=64):
            for s in range(2):
                load_scale_rows(queue, plane, src, col0, width, s, base)

        def spread_scale_pairs(plane, col0, width):
            nc.vector.tensor_copy(
                plane[0:64, 1, col0 : col0 + width].bitcast(I32),
                plane[64:128, 0, col0 : col0 + width].bitcast(I32),
            )

        def load_column(src, name):
            dst = tile([P, ROW_TILES], F32, name)
            with nc.allow_non_contiguous_dma(reason="one value a partition"):
                nc.sync.dma_start(dst[:], src.rearrange("(c p) o -> p (c o)", p=P))
            return dst

        plane_w = tile([P, 2, R], U8, "plane_w")
        plane_b = tile([P, 2, 2 * R], U8, "plane_b")
        plane_c = tile([P, 2, 2 * N], U8, "plane_c")
        xt_stage = tile([P, 2, T], U8, "xt_stage")
        xo_stage = keep.tile([P, 2, Z], U8, name="xo_stage", tag="xo_stage", align_bytes=64)
        xt_plane = tile([P, T], U8, "xt_plane")
        xo_plane = tile([P, Z], U8, "xo_plane")
        board = [tile([P, C], F32, "board%d" % n) for n in range(ROW_TILES)]
        ident = tile([P, P], F32, "ident")
        warm_in = tile([P, 1], F32, "warm_in")
        warm_out = tile([P, 1], F32, "warm_out")
        nc.vector.memset(xt_stage[0:64, 0, :].bitcast(I32), 0)
        nc.gpsimd.memset(xt_stage[0:64, 1, :].bitcast(I32), 0)
        nc.vector.memset(plane_w[64:128].bitcast(I32), 0)
        nc.gpsimd.memset(plane_b[64:128, :, R : 2 * R].bitcast(I32), 0)
        nc.vector.memset(plane_b[64:128, :, 0:R].bitcast(I32), 0)
        nc.vector.memset(xo_stage[0:64].bitcast(I32), 0)
        nc.vector.memset(board[0][:], 0.0)
        nc.vector.memset(warm_in[:], 0.0)
        load_scale_rows(nc.gpsimd, plane_b, w0_scales, R, R, 1)
        nc.gpsimd.memset(plane_c[64:128].bitcast(I32), 0)
        make_identity(nc, ident[:])
        nc.gpsimd.memset(board[1][:], 0.0)
        nc.scalar.activation(warm_out[:], warm_in[:], ACT.Sigmoid)

        idx = load_list(offs, "idx")
        w_tab = load_words(nc.sync, w_words, 2 * R, U8, "w_tab")
        load_scale_pairs(nc.sync, xt_stage, xt_scales, 0, T, base=0)
        load_scale_pairs(nc.sync, plane_w, w_scales, 0, R)
        load_scale_rows(nc.sync, plane_b, w2_scales, 0, R, 0)
        xt_tab = load_words(nc.sync, xt_words, T, U32, "xt_tab")
        load_scale_rows(nc.sync, plane_b, w2_scales, 0, R, 1)
        xo_tab = load_words(nc.sync, xo_words, Z, U16, "xo_tab")
        load_scale_rows(nc.sync, plane_b, w0_scales, R, R, 0)
        idx2 = load_list(offs2, "idx2")
        w2_tab = load_words(nc.sync, w2_words, R, U32, "w2_tab")
        load_scale_pairs(nc.sync, xo_stage, xo_scales, 0, Z, base=0)
        w0_tab = load_words(nc.sync, w0_words, R, U32, "w0_tab")
        load_scale_pairs(nc.sync, plane_c, wb_scales, 0, N)
        load_scale_pairs(nc.sync, plane_c, wc_scales, N, N)
        wb_tab = load_words(nc.sync, wb_words, N, U32, "wb_tab")
        idx3 = load_list(offs3, "idx3")
        wc_tab = load_words(nc.sync, wc_words, 2 * N, U8, "wc_tab")
        idx6 = load_list(offs6, "idx6")
        sp_col = load_column(sp, "sp_col")
        bo_col = load_column(bo, "bo_col")
        idx5 = load_list(offs5, "idx5")
        so_col = load_column(so, "so_col")
        idx4 = load_list(offs4, "idx4")

        def spread_table_scales(plane, stage):
            for c in range(2):
                nc.vector.tensor_copy(plane[64 * c : 64 * c + 64, :].bitcast(I32), stage[0:64, c, :].bitcast(I32))

        spread_table_scales(xt_plane, xt_stage)
        xt_codes = [tile([P, P], U32, "xt_codes%d" % h) for h in range(HALVES)]
        xt_bytes = [tile([P, P], U8, "xt_bytes%d" % h) for h in range(HALVES)]
        xo_bytes = [tile([P, P], U8, "xo_bytes%d" % h) for h in range(HALVES)]

        def half(lst, h):
            return lst[:, 8 * h : 8 * h + 8]

        bank_a = [psum.tile([P, R], F32, name="bank_a%d" % h) for h in range(HALVES)]
        bank_b = [psum.tile([P, R], F32, name="bank_b%d" % h) for h in range(HALVES)]
        bank_p = [psum.tile([P, J], F32, name="bank_p%d" % n) for n in range(ROW_TILES)]
        bank_q = [psum.tile([P, J], F32, name="bank_q%d" % n) for n in range(ROW_TILES)]
        a_rows = [tile([P, R], F32, "a_rows%d" % h) for h in range(HALVES)]

        def by_word_planes(bank):
            return bank[:].rearrange("j (p u e) -> j u p e", u=2, e=2)

        def as_word_planes(t):
            return t[:].rearrange("j (u p e) -> j u p e", u=2, e=2)

        for h in range(HALVES):
            nc.vector.tensor_copy(xt_bytes[h][:], xt_plane[:].indirect(half(idx, h)))
            nc.vector.tensor_copy(xt_codes[h][:], xt_tab[:].indirect(half(idx, h)))
            if h == 0:
                spread_scale_pairs(plane_w, 0, R)
            nc.tensor.matmul_mx(
                bank_a[h][:], lhsT=xt_codes[h][:].bitcast(E4M3), lhsT_scale=xt_bytes[h][:],
                rhs=w_tab[:].bitcast(E2M1), rhs_scale=plane_w[:, 1, 0:R], start=True, stop=True,
            )
            nc.scalar.copy(as_word_planes(a_rows[h]), by_word_planes(bank_a[h]))
        spread_scale_pairs(plane_b, 0, 2 * R)
        xo_codes = [tile([P, P], U16, "xo_codes0")]
        nc.vector.tensor_copy(xo_codes[0][:], xo_tab[:].indirect(half(idx2, 0)))
        spread_table_scales(xo_plane, xo_stage)
        xo_codes.append(keep.tile([P, P], U16, name="xo_codes1", tag="xo_stage", align_bytes=64))
        for h in range(HALVES):
            nc.tensor.matmul_mx(
                bank_b[h][:], lhsT=xt_codes[h][:].bitcast(E4M3), lhsT_scale=xt_bytes[h][:],
                rhs=w2_tab[:].bitcast(E5M2), rhs_scale=plane_b[:, 1, 0:R], start=True, stop=False,
            )
        for h in range(HALVES):
            nc.vector.tensor_copy(xo_bytes[h][:], xo_plane[:].indirect(half(idx2, h)))
            if h == 1:
                nc.vector.tensor_copy(xo_codes[h][:], xo_tab[:].indirect(half(idx2, h)))
            nc.tensor.matmul_mx(
                bank_b[h][:], lhsT=xo_codes[h][:].bitcast(E2M1), lhsT_scale=xo_bytes[h][:],
                rhs=w0_tab[:].bitcast(E5M2), rhs_scale=plane_b[:, 1, R : 2 * R], start=False, stop=True,
            )

        hid_rows = [tile([P, R], BF16, "hid_rows%d" % h) for h in range(HALVES)]
        hid_cols = [tile([P, R], BF16, "hid_cols%d" % h) for h in range(HALVES)]
        hid_codes = [tile([P, P], U32, "hid_codes%d" % h) for h in range(HALVES)]
        hid_bytes = [tile([P, P], U8, "hid_bytes%d" % h) for h in range(HALVES)]
        for h in range(HALVES):
            words = hid_rows[h][:].bitcast(F32)
            for u in range(2):
                nc.vector.tensor_tensor(
                    as_word_planes(hid_rows[h])[:, u], by_word_planes(bank_b[h])[:, u],
                    as_word_planes(a_rows[h])[:, u], ALU.max,
                )
                nc.tensor.transpose(bank_a[h][:, u * P : (u + 1) * P], words[:, u * P : (u + 1) * P], ident[:])
            nc.scalar.copy(
                hid_cols[h][:].bitcast(F32).rearrange("p (j u) -> p j u", u=2),
                bank_a[h][:, 0 : 2 * P].rearrange("p (u j) -> p j u", u=2),
            )
        spread_scale_pairs(plane_c, 0, 2 * N)

        p_rows = [tile([P, J], F32, "p_rows%d" % n) for n in range(ROW_TILES)]
        for h in range(HALVES):
            cols = slice(h * P, (h + 1) * P)
            nc.vector.quantize_mx(out=hid_codes[h][:].bitcast(E4M3), scales=hid_bytes[h][:], in_=hid_cols[h][:])
            for n in range(ROW_TILES):
                nc.tensor.matmul_mx(
                    bank_p[n][:, cols], lhsT=wb_tab[:, n * P : (n + 1) * P].bitcast(E5M2),
                    lhsT_scale=plane_c[:, 1, n * P : (n + 1) * P],
                    rhs=hid_codes[h][:].bitcast(E4M3), rhs_scale=hid_bytes[h][:], start=True, stop=True,
                )
            nc.vector.tensor_copy(p_rows[0][:, cols], bank_p[0][:, cols])
            nc.scalar.copy(p_rows[1][:, cols], bank_p[1][:, cols])
            for n in range(ROW_TILES):
                nc.tensor.matmul_mx(
                    bank_q[n][:, cols], lhsT=wc_tab[:, 2 * n * P : 2 * (n + 1) * P].bitcast(E2M1),
                    lhsT_scale=plane_c[:, 1, N + n * P : N + (n + 1) * P],
                    rhs=hid_codes[h][:].bitcast(E4M3), rhs_scale=hid_bytes[h][:], start=True, stop=True,
                )
        for h in range(HALVES):
            cols = slice(h * P, (h + 1) * P)
            nc.vector.tensor_copy(board[0][:].indirect(half(idx3, h)), p_rows[0][:, cols])
            nc.scalar.activation(board[1][:].indirect(half(idx3, h)), p_rows[1][:, cols], ACT.Copy)

        picked = [tile([P, J], F32, "picked%d" % n) for n in range(ROW_TILES)]
        kept = [tile([P, J], F32, "kept%d" % n) for n in range(ROW_TILES)]
        for n in range(ROW_TILES):
            nc.vector.tensor_copy(picked[n][:, 0:P], board[n][:].indirect(half(idx4, 0)))
            nc.scalar.activation(picked[n][:, P:J], board[n][:].indirect(half(idx4, 1)), ACT.Copy)
        for n in range(ROW_TILES):
            nc.vector.tensor_tensor(kept[n][:], picked[n][:], bank_q[n][:], ALU.max)
        for n in range(ROW_TILES):
            gate = tile([P, O], F32, "gate%d" % n)
            scaled = tile([P, O], F32, "scaled%d" % n)
            result = tile([P, O], F32, "result%d" % n)
            nc.scalar.activation(
                gate[:], kept[n][:].indirect(idx6[:]), ACT.Sigmoid,
                bias=bo_col[:, n : n + 1], scale=sp_col[:, n : n + 1],
            )
            nc.scalar.activation(scaled[:], kept[n][:].indirect(idx5[:]), ACT.Copy, scale=so_col[:, n : n + 1])
            nc.vector.tensor_tensor(result[:], scaled[:], gate[:], ALU.mult)
            nc.sync.dma_start(out[n * P : (n + 1) * P, :], result[:])
